import numpy as np
import ml_dtypes


def mxq(x, axis, fmt="e4m3"):
    dtype, down = {"e4m3": (ml_dtypes.float8_e4m3fn, 7), "e5m2": (ml_dtypes.float8_e5m2, 14)}[fmt]
    v = np.moveaxis(np.asarray(x, np.float32).astype(ml_dtypes.bfloat16).astype(np.float64), axis, -1)
    blocks = v.reshape(v.shape[:-1] + (-1, 32))
    amax = np.abs(blocks).max(-1, keepdims=True)
    byte = np.maximum(np.where(amax > 0, np.frexp(amax)[1] - 1 + 127, 0) - down, 1)
    scale = np.exp2(byte - 127.0)
    codes = (blocks / scale).astype(np.float32).astype(dtype).astype(np.float64)
    return np.moveaxis((codes * scale).reshape(v.shape), -1, axis)


WIDE = False


def mx_kscale(k):
    if not WIDE:
        return np.ones(k)
    levels = np.array([10, -10, 5, -5, 0])
    if k % 512:
        return np.exp2(np.random.permutation(np.resize(levels, k // 32))).repeat(32)
    a = np.empty((k // 512, 16))
    for p in range(k // 512):
        a[p, :8] = np.random.permutation(np.resize(levels, 8))
        for g in range(8):
            far = levels[np.abs(levels - a[p, g]) >= 10]
            a[p, g + 8] = far[np.random.randint(len(far))]
    return np.exp2(a.ravel()).repeat(32)


def f64(x):
    return np.asarray(x).astype(np.float64)


def striped(idx):
    return np.tile(idx.reshape(-1, 16).T, (8, 1)).astype(np.uint16)


def unstriped(offs):
    return offs[:16].T.reshape(-1).astype(np.int64)


def striped8(idx):
    return np.concatenate([x.reshape(-1, 16).T for x in idx]).astype(np.uint16)


def runs(offs, k):
    lists = np.stack([offs[16 * r : 16 * r + 16].T.reshape(-1) for r in range(8)]).astype(np.int64)
    return lists[np.arange(k) % 512 // 64]


def pack_weight(w):
    k, n = w.shape
    w = f64(np.asarray(w, np.float32).astype(ml_dtypes.bfloat16)).reshape(k // 32, 32, n)
    amax = np.abs(w).max(1)
    byte = np.clip(np.where(amax > 0, np.frexp(amax)[1] - 1 + 127 - 7, 1), 1, 254)
    scaled = (w * np.exp2(127.0 - byte)[:, None, :]).reshape(k, n).astype(np.float32)
    words = np.ascontiguousarray(scaled.reshape(k // 512, 128, 4, n).transpose(0, 1, 3, 2)).astype(ml_dtypes.float8_e4m3fn).view(np.uint8)
    return words, np.ascontiguousarray(byte.astype(np.uint8).reshape(k // 512, 16, n))


def unpack_weight(words, scales):
    g, p, n, _ = words.shape
    vals = np.ascontiguousarray(words).view(ml_dtypes.float8_e4m3fn).astype(np.float64) * np.repeat(np.exp2(scales.astype(np.float64) - 127.0), 8, axis=1)[..., None]
    return vals.transpose(0, 1, 3, 2).reshape(g * 512, n)


def sigmoid(v):
    return 1.0 / (1.0 + np.exp(-np.maximum(v, -700.0)))


K, T, S, N, H = 512, 2048, 512, 512, 512


def setup_inputs():
    n = np.random.standard_normal
    s = mx_kscale(K)[:, None]
    u = mx_kscale(S)
    packed_xT = pack_weight(n((K, T)) * s)
    return {
        "x_words": packed_xT[0],
        "x_scales": packed_xT[1],
        "wa": (n((K, H)) / np.sqrt(K) / s).astype(np.float32),
        "wb": (n((K, H)) / np.sqrt(K) / s).astype(np.float32),
        "gt": (np.random.uniform(0.5, 1.5, (S, 1)) * u[:, None]).astype(np.float32),
        "w1": (n((S, N)) / np.sqrt(S) / u[:, None]).astype(np.float32),
        "offs": striped(np.random.permutation(T)[:S]),
        "two": striped(np.random.permutation(T)[:S]),
        "n1": striped8(np.stack([np.random.permutation(H) for _ in range(8)])),
        "n2": striped8(np.stack([np.random.permutation(H) for _ in range(8)])),
        "n3": striped8(np.stack([np.random.permutation(H) for _ in range(8)])),
    }


def reference(x_words, x_scales, wa, wb, gt, w1, offs, two, n1, n2, n3):
    xq = unpack_weight(x_words, x_scales)[:, unstriped(offs)]
    y = xq.T @ mxq(f64(wa), 0, "e4m3")
    x_two = unpack_weight(x_words, x_scales)[:, unstriped(two)]
    d = x_two.T @ mxq(f64(wb), 0, "e4m3")
    z = f64(gt) * (y * (sigmoid(d[np.arange(S)[:, None], runs(n2, S)])) - (0.5 * (y[np.arange(S)[:, None], runs(n1, S)])))
    h = mxq(f64(w1), 0, "e4m3").T @ mxq(z, 0, "e4m3")
    return h - (h[np.arange(N)[:, None], runs(n3, N)])

@@ -1,0 +1,210 @@
+from contextlib import ExitStack
+
+import concourse.mybir as mybir
+
+K, T, S, N, H = 512, 2048, 512, 512, 512
+FLOPS = 2 * (K * S * H + K * S * H + S * N * H)
+
+F32 = mybir.dt.float32
+BF16 = mybir.dt.bfloat16
+I32 = mybir.dt.int32
+U32 = mybir.dt.uint32
+U16 = mybir.dt.uint16
+U8 = mybir.dt.uint8
+FP8X4 = mybir.dt.float8_e4m3fn_x4
+ALU = mybir.AluOpType
+ACT = mybir.ActivationFunctionType
+
+P = 128
+PACK = 4
+RUN = 8
+BLOCKS = P // RUN
+HALF = H // 2
+LIST_COLS = HALF // 16
+
+
+def tile_picked_twtgatebdif_none_p_kernel(
+    tc, x_words, x_scales, wa, wb, gt, w1, offs, two, n1, n2, n3, out
+):
+    nc = tc.nc
+    with ExitStack() as ctx:
+        sb = ctx.enter_context(tc.tile_pool(name="sb", bufs=1))
+        psum = ctx.enter_context(tc.psum_pool(name="psum", bufs=1))
+
+        def tile(name, shape, dtype, tag="", bufs=1):
+            return sb.tile(shape, dtype, name=name, tag=tag or name, bufs=bufs, align_bytes=64)
+
+        def bank(b, width):
+            return psum.tile([P, width], F32, name="bank%d" % b)
+
+        def half(c):
+            return slice(c * HALF, (c + 1) * HALF)
+
+        def load_list(name, src):
+            lst = tile(name, [P, S // 16], U16)
+            nc.sync.dma_start(lst[:], src)
+            return lst
+
+        def load_weight(name, src):
+            halves = [tile("%s%d" % (name, c), [P, PACK, HALF], F32) for c in range(2)]
+            for c in range(2):
+                nc.sync.dma_start(halves[c][:], src.rearrange("(p j) n -> p j n", j=PACK)[:, :, half(c)])
+            return halves
+
+        def list_half(lst, c):
+            return lst[:, c * LIST_COLS : (c + 1) * LIST_COLS]
+
+        two_l = load_list("two_l", two)
+        xs = tile("xs", [P, T], U8)
+        for q in range(4):
+            rows = x_scales[0, 4 * q : 4 * q + 4, :].bitcast(I32)
+            nc.sync.dma_start(xs[32 * q : 32 * (q + 1), :].bitcast(I32), rows.unsqueeze(0).broadcast_to([8, 4, T // 4]))
+        warm = tile("warm", [P, 8], F32)
+        nc.vector.memset(warm[:], 0.0)
+        warm_out = tile("warm_out", [P, 8], F32)
+        nc.scalar.activation(warm_out[:], warm[:], ACT.Sigmoid)
+
+        offs_l = load_list("offs_l", offs)
+        xw = tile("xw", [P, T], I32)
+        nc.sync.dma_start(xw[:], x_words[0].rearrange("p n t -> p (n t)").bitcast(I32))
+        wb_raw = load_weight("wb_raw", wb)
+        n2_l = load_list("n2_l", n2)
+        wa_raw = load_weight("wa_raw", wa)
+        n1_l = load_list("n1_l", n1)
+        gt_rows = gt.rearrange("(b t q) o -> t b q o", t=PACK, q=RUN)
+        gt_col = [tile("gt_col%d" % t, [P, 1], F32) for t in range(PACK)]
+        for t in range(PACK):
+            nc.sync.dma_start(gt_col[t][:], gt_rows[t])
+        w1_raw = tile("w1_raw", [P, PACK, N], F32)
+        w1_rows = w1.rearrange("(b t q) m -> t b q m", t=PACK, q=RUN)
+        for t in range(PACK):
+            nc.sync.dma_start(w1_raw[:, t, :], w1_rows[t])
+        n3_l = load_list("n3_l", n3)
+
+        def pick_scales(name, lst):
+            picked = tile(name + "_picked", [P, S], U8)
+            nc.vector.tensor_copy(picked[:], xs[:].indirect(lst[:]))
+            dealt = tile(name, [P, S], U8)
+            nc.vector.tensor_copy(
+                dealt[:].bitcast(I32).rearrange("p (t b e) -> p t b e", t=PACK, b=BLOCKS),
+                picked[:].bitcast(I32).rearrange("p (b t e) -> p t b e", t=PACK, b=BLOCKS),
+            )
+            return dealt
+
+        def pick_words(name, lst):
+            dealt = tile(name, [P, S], U32)
+            nc.vector.tensor_copy(
+                dealt[:].rearrange("p (t b q) -> p b t q", t=PACK, b=BLOCKS),
+                xw[:].bitcast(U32).indirect(lst[:]),
+            )
+            return dealt
+
+        def interleave(copy, dst, src):
+            copy(
+                dst.rearrange("p (c i) t -> p c t i", i=4),
+                src.rearrange("p t (c i) -> p c t i", i=4),
+            )
+
+        def quantize(codes, scales, grouped):
+            nc.vector.quantize_mx(out=codes.bitcast(FP8X4), scales=scales, in_=grouped.rearrange("p w j -> p (w j)"))
+
+        def quantize_weight(name, raw, copies):
+            codes = tile(name + "_codes", [P, H], U32)
+            scales = tile(name + "_scales", [P, H], U8)
+            grouped = [tile("%s_grouped%d" % (name, c), [P, HALF, PACK], BF16) for c in range(2)]
+            for c in range(2):
+                interleave(copies[c], grouped[c][:], raw[c][:])
+            for c in range(2):
+                quantize(codes[:, half(c)], scales[:, half(c)], grouped[c][:])
+            return codes, scales
+
+        def product(acc, lhs_codes, lhs_scales, t, rhs_codes, rhs_scales):
+            cols = slice(t * P, (t + 1) * P)
+            nc.tensor.matmul_mx(
+                out=acc, lhsT=lhs_codes[:, cols].bitcast(FP8X4), lhsT_scale=lhs_scales[:, cols],
+                rhs=rhs_codes.bitcast(FP8X4), rhs_scale=rhs_scales, start=True, stop=True,
+            )
+
+        two_scales = pick_scales("two_scales", two_l)
+        offs_scales = pick_scales("offs_scales", offs_l)
+        two_words = pick_words("two_words", two_l)
+        offs_words = pick_words("offs_words", offs_l)
+        wb_codes, wb_scales = quantize_weight("wb", wb_raw, (nc.scalar.copy, nc.scalar.copy))
+        d_ps = [bank(t, H) for t in range(PACK)]
+        for t in range(PACK):
+            product(d_ps[t][:], two_words, two_scales, t, wb_codes[:], wb_scales[:])
+        wa_codes, wa_scales = quantize_weight("wa", wa_raw, (nc.scalar.copy, nc.vector.tensor_copy))
+        y_ps = [bank(PACK + t, H) for t in range(PACK)]
+        for t in range(PACK):
+            product(y_ps[t][:], offs_words, offs_scales, t, wa_codes[:], wa_scales[:])
+
+        w1_codes = tile("w1_codes", [P, N], U32)
+        w1_scales = tile("w1_scales", [P, N], U8)
+
+        def cast_w1(c):
+            dst = w1_grouped[:].rearrange("p (u m) t -> p m t u", u=PACK)
+            src = w1_raw[:].rearrange("p t (m u) -> p m t u", u=PACK)
+            nc.scalar.copy(dst[:, 64 * c : 64 * (c + 1)], src[:, 64 * c : 64 * (c + 1)])
+
+        def halve_on_scalar(dst, src):
+            nc.scalar.activation(dst, src, ACT.Copy, scale=-0.5)
+
+        def halve_on_vector(dst, src):
+            nc.vector.tensor_scalar(dst, src, -0.5, None, ALU.mult)
+
+        z = [tile("z%d" % c, [P, PACK, HALF], F32) for c in range(2)]
+        d_sb = [tile("d_sb%d" % t, [P, H], F32) for t in range(PACK)]
+        y_sb = [tile("y_sb%d" % t, [P, H], F32) for t in range(PACK)]
+        h_neg = [tile("h_neg%d" % u, [P, H], F32) for u in range(PACK)]
+        h_pos = [[tile("h_pos%d_%d" % (u, c), [P, HALF], F32) for c in range(2)] for u in range(PACK)]
+
+        def mix(t, c):
+            sig = tile("sig%d_%d" % (t, c), [P, HALF], F32, tag="sig", bufs=3)
+            if c == 0:
+                nc.scalar.copy(d_sb[t][:], d_ps[t][:])
+            nc.scalar.activation(sig[:], d_sb[t][:].indirect(list_half(n2_l, c)), ACT.Sigmoid)
+            if c == 0 and t < 2:
+                nc.vector.tensor_scalar(y_sb[t][:], y_ps[t][:], gt_col[t][:], None, ALU.mult)
+            elif c == 0:
+                nc.scalar.activation(y_sb[t][:], y_ps[t][:], ACT.Copy, scale=gt_col[t][:])
+            gated = tile("gated%d_%d" % (t, c), [P, HALF], F32)
+            nc.vector.scalar_tensor_tensor(gated[:], y_sb[t][:, half(c)], 2.0, sig[:], ALU.mult, ALU.mult)
+            nc.vector.tensor_tensor(z[c][:, t, :], y_sb[t][:].indirect(list_half(n1_l, c)), gated[:], ALU.subtract)
+
+        z_codes = [tile("z_codes%d" % c, [P, HALF], U32) for c in range(2)]
+        z_scales = [tile("z_scales%d" % c, [P, HALF], U8) for c in range(2)]
+
+        for c in range(2):
+            for t in range(PACK):
+                mix(t, c)
+        w1_grouped = tile("w1_grouped", [P, N, PACK], BF16, tag="d_sb3")
+        cast_w1(0)
+        cast_w1(1)
+        z_grouped = [
+            tile("z_grouped0", [P, HALF, PACK], BF16, tag="sig", bufs=3),
+            tile("z_grouped1", [P, HALF, PACK], BF16),
+        ]
+        interleave(halve_on_scalar, z_grouped[0][:], z[0][:])
+        interleave(halve_on_vector, z_grouped[1][:], z[1][:])
+        quantize(z_codes[1][:], z_scales[1][:], z_grouped[1][:])
+        quantize(w1_codes[:], w1_scales[:], w1_grouped[:])
+        quantize(z_codes[0][:], z_scales[0][:], z_grouped[0][:])
+        for u in range(PACK):
+            h_ps = [bank(PACK * c + u, HALF) for c in range(2)]
+            for c in range(2):
+                product(h_ps[c][:], w1_codes, w1_scales, u, z_codes[c][:], z_scales[c][:])
+            for c in range(2):
+                nc.scalar.activation(h_neg[u][:, half(c)], h_ps[c][:], ACT.Copy, scale=-1.0)
+            for c in range(2):
+                copy = nc.vector.tensor_copy if (u, c) == (0, 0) else nc.scalar.copy
+                copy(h_pos[u][c][:], h_ps[c][:])
+
+        out_rows = out.rearrange("(p u) n -> u p n", u=PACK)
+        for u in range(PACK):
+            res = tile("res%d" % u, [P, H], F32)
+            for c in range(2):
+                nc.vector.tensor_tensor(res[:, half(c)], h_neg[u][:].indirect(list_half(n3_l, c)), h_pos[u][c][:], ALU.add)
+                if u == PACK - 1:
+                    nc.sync.dma_start(out_rows[u][:, half(c)], res[:, half(c)])
+            if u < PACK - 1:
+                nc.sync.dma_start(out_rows[u], res[:])

@@ -74,7 +74,7 @@ def tile_picked_twtgatebdif_none_p_kernel(
         gt_rows = gt.rearrange("(b t q) o -> t b q o", t=PACK, q=RUN)
         gt_col = [tile("gt_col%d" % t, [P, 1], F32) for t in range(PACK)]
         for t in range(PACK):
-            nc.sync.dma_start(gt_col[t][:], gt_rows[t])
+            nc.gpsimd.dma_start(gt_col[t][:], gt_rows[t])
         w1_raw = tile("w1_raw", [P, PACK, N], F32)
         w1_rows = w1.rearrange("(b t q) m -> t b q m", t=PACK, q=RUN)
         for t in range(PACK):
@@ -84,6 +84,9 @@ def tile_picked_twtgatebdif_none_p_kernel(
         def pick_scales(name, lst):
             picked = tile(name + "_picked", [P, S], U8)
             nc.vector.tensor_copy(picked[:], xs[:].indirect(lst[:]))
+            return picked
+
+        def deal_scales(name, picked):
             dealt = tile(name, [P, S], U8)
             nc.vector.tensor_copy(
                 dealt[:].bitcast(I32).rearrange("p (t b e) -> p t b e", t=PACK, b=BLOCKS),
@@ -125,8 +128,10 @@ def tile_picked_twtgatebdif_none_p_kernel(
                 rhs=rhs_codes.bitcast(FP8X4), rhs_scale=rhs_scales, start=True, stop=True,
             )
 
-        two_scales = pick_scales("two_scales", two_l)
-        offs_scales = pick_scales("offs_scales", offs_l)
+        two_picked = pick_scales("two_scales", two_l)
+        offs_picked = pick_scales("offs_scales", offs_l)
+        two_scales = deal_scales("two_scales", two_picked)
+        offs_scales = deal_scales("offs_scales", offs_picked)
         two_words = pick_words("two_words", two_l)
         offs_words = pick_words("offs_words", offs_l)
         wb_codes, wb_scales = quantize_weight("wb", wb_raw, (nc.scalar.copy, nc.scalar.copy))
@@ -138,14 +143,6 @@ def tile_picked_twtgatebdif_none_p_kernel(
         for t in range(PACK):
             product(y_ps[t][:], offs_words, offs_scales, t, wa_codes[:], wa_scales[:])
 
-        w1_codes = tile("w1_codes", [P, N], U32)
-        w1_scales = tile("w1_scales", [P, N], U8)
-
-        def cast_w1(c):
-            dst = w1_grouped[:].rearrange("p (u m) t -> p m t u", u=PACK)
-            src = w1_raw[:].rearrange("p t (m u) -> p m t u", u=PACK)
-            nc.scalar.copy(dst[:, 64 * c : 64 * (c + 1)], src[:, 64 * c : 64 * (c + 1)])
-
         def halve_on_scalar(dst, src):
             nc.scalar.activation(dst, src, ACT.Copy, scale=-0.5)
 
@@ -155,56 +152,72 @@ def tile_picked_twtgatebdif_none_p_kernel(
         z = [tile("z%d" % c, [P, PACK, HALF], F32) for c in range(2)]
         d_sb = [tile("d_sb%d" % t, [P, H], F32) for t in range(PACK)]
         y_sb = [tile("y_sb%d" % t, [P, H], F32) for t in range(PACK)]
-        h_neg = [tile("h_neg%d" % u, [P, H], F32) for u in range(PACK)]
-        h_pos = [[tile("h_pos%d_%d" % (u, c), [P, HALF], F32) for c in range(2)] for u in range(PACK)]
 
-        def mix(t, c):
+        def gate(t, c):
             sig = tile("sig%d_%d" % (t, c), [P, HALF], F32, tag="sig", bufs=3)
             if c == 0:
                 nc.scalar.copy(d_sb[t][:], d_ps[t][:])
             nc.scalar.activation(sig[:], d_sb[t][:].indirect(list_half(n2_l, c)), ACT.Sigmoid)
-            if c == 0 and t < 2:
-                nc.vector.tensor_scalar(y_sb[t][:], y_ps[t][:], gt_col[t][:], None, ALU.mult)
-            elif c == 0:
+            if c == 0 and t >= 2:
                 nc.scalar.activation(y_sb[t][:], y_ps[t][:], ACT.Copy, scale=gt_col[t][:])
             gated = tile("gated%d_%d" % (t, c), [P, HALF], F32)
             nc.vector.scalar_tensor_tensor(gated[:], y_sb[t][:, half(c)], 2.0, sig[:], ALU.mult, ALU.mult)
+            return gated
+
+        def subtract(t, c, gated):
             nc.vector.tensor_tensor(z[c][:, t, :], y_sb[t][:].indirect(list_half(n1_l, c)), gated[:], ALU.subtract)
 
-        z_codes = [tile("z_codes%d" % c, [P, HALF], U32) for c in range(2)]
-        z_scales = [tile("z_scales%d" % c, [P, HALF], U8) for c in range(2)]
+        for t in range(2):
+            nc.vector.tensor_scalar(y_sb[t][:], y_ps[t][:], gt_col[t][:], None, ALU.mult)
+        steps = [(t, c) for c in range(2) for t in range(PACK)]
+        gated = [gate(*steps[0])]
+        for k in range(1, len(steps)):
+            gated.append(gate(*steps[k]))
+            subtract(*steps[k - 1], gated[k - 1])
+        subtract(*steps[-1], gated[-1])
 
-        for c in range(2):
-            for t in range(PACK):
-                mix(t, c)
-        w1_grouped = tile("w1_grouped", [P, N, PACK], BF16, tag="d_sb3")
-        cast_w1(0)
-        cast_w1(1)
         z_grouped = [
             tile("z_grouped0", [P, HALF, PACK], BF16, tag="sig", bufs=3),
             tile("z_grouped1", [P, HALF, PACK], BF16),
         ]
+        z_codes = [tile("z_codes%d" % c, [P, HALF], U32) for c in range(2)]
+        z_scales = [tile("z_scales%d" % c, [P, HALF], U8) for c in range(2)]
+        w1_grouped = tile("w1_grouped", [P, N, PACK], BF16, tag="d_sb3")
+        w1_codes = tile("w1_codes", [P, N], U32)
+        w1_scales = tile("w1_scales", [P, N], U8)
+
+        def quantize_w1(u):
+            cols = slice(u * P, (u + 1) * P)
+            nc.scalar.copy(
+                w1_grouped[:, cols, :].rearrange("p (b c i) t -> p b c t i", c=2, i=4),
+                w1_raw[:].rearrange("p t (b u c i) -> p u b c t i", u=PACK, c=2, i=4)[:, u],
+            )
+            quantize(w1_codes[:, cols], w1_scales[:, cols], w1_grouped[:, cols, :])
+
         interleave(halve_on_scalar, z_grouped[0][:], z[0][:])
-        interleave(halve_on_vector, z_grouped[1][:], z[1][:])
-        quantize(z_codes[1][:], z_scales[1][:], z_grouped[1][:])
-        quantize(w1_codes[:], w1_scales[:], w1_grouped[:])
         quantize(z_codes[0][:], z_scales[0][:], z_grouped[0][:])
+        quantize_w1(0)
+        interleave(halve_on_vector, z_grouped[1][:], z[1][:])
+        quantize_w1(1)
+        quantize(z_codes[1][:], z_scales[1][:], z_grouped[1][:])
+
+        out_rows = out.rearrange("(b u q) n -> u b q n", u=PACK, q=RUN)
         for u in range(PACK):
+            h_neg = tile("h_neg%d" % u, [P, H], F32)
+            h_pos = [tile("h_pos%d_%d" % (u, c), [P, HALF], F32) for c in range(2)]
             h_ps = [bank(PACK * c + u, HALF) for c in range(2)]
             for c in range(2):
                 product(h_ps[c][:], w1_codes, w1_scales, u, z_codes[c][:], z_scales[c][:])
             for c in range(2):
-                nc.scalar.activation(h_neg[u][:, half(c)], h_ps[c][:], ACT.Copy, scale=-1.0)
+                nc.scalar.activation(h_neg[:, half(c)], h_ps[c][:], ACT.Copy, scale=-1.0)
             for c in range(2):
-                copy = nc.vector.tensor_copy if (u, c) == (0, 0) else nc.scalar.copy
-                copy(h_pos[u][c][:], h_ps[c][:])
-
-        out_rows = out.rearrange("(p u) n -> u p n", u=PACK)
-        for u in range(PACK):
+                nc.scalar.copy(h_pos[c][:], h_ps[c][:])
+            if u + 2 < PACK:
+                quantize_w1(u + 2)
             res = tile("res%d" % u, [P, H], F32)
             for c in range(2):
-                nc.vector.tensor_tensor(res[:, half(c)], h_neg[u][:].indirect(list_half(n3_l, c)), h_pos[u][c][:], ALU.add)
+                nc.vector.tensor_tensor(res[:, half(c)], h_neg[:].indirect(list_half(n3_l, c)), h_pos[c][:], ALU.add)
                 if u == PACK - 1:
-                    nc.sync.dma_start(out_rows[u][:, half(c)], res[:, half(c)])
+                    nc.sync.dma_start(out_rows[u][:, :, half(c)], res[:, half(c)])
             if u < PACK - 1:
                 nc.sync.dma_start(out_rows[u], res[:])

@@ -55,26 +55,27 @@ def tile_picked_twtgatebdif_none_p_kernel(
             return lst[:, c * LIST_COLS : (c + 1) * LIST_COLS]
 
         two_l = load_list("two_l", two)
+        offs_l = load_list("offs_l", offs)
+        n2_l = load_list("n2_l", n2)
         xs = tile("xs", [P, T], U8)
-        for q in range(4):
-            rows = x_scales[0, 4 * q : 4 * q + 4, :].bitcast(I32)
-            nc.sync.dma_start(xs[32 * q : 32 * (q + 1), :].bitcast(I32), rows.unsqueeze(0).broadcast_to([8, 4, T // 4]))
+        nc.vector.memset(xs[:].bitcast(I32), 0)
+        scale_rows = x_scales[0].bitcast(I32).rearrange("(q r) c -> r q c", r=4)
+        for r in range(4):
+            nc.sync.dma_start(xs[r:P:32, :].bitcast(I32), scale_rows[r])
         warm = tile("warm", [P, 8], F32)
         nc.vector.memset(warm[:], 0.0)
         warm_out = tile("warm_out", [P, 8], F32)
         nc.scalar.activation(warm_out[:], warm[:], ACT.Sigmoid)
 
-        offs_l = load_list("offs_l", offs)
         xw = tile("xw", [P, T], I32)
         nc.sync.dma_start(xw[:], x_words[0].rearrange("p n t -> p (n t)").bitcast(I32))
         wb_raw = load_weight("wb_raw", wb)
-        n2_l = load_list("n2_l", n2)
         wa_raw = load_weight("wa_raw", wa)
         n1_l = load_list("n1_l", n1)
         gt_rows = gt.rearrange("(b t q) o -> t b q o", t=PACK, q=RUN)
         gt_col = [tile("gt_col%d" % t, [P, 1], F32) for t in range(PACK)]
         for t in range(PACK):
-            nc.gpsimd.dma_start(gt_col[t][:], gt_rows[t])
+            nc.sync.dma_start(gt_col[t][:], gt_rows[t])
         w1_raw = tile("w1_raw", [P, PACK, N], F32)
         w1_rows = w1.rearrange("(b t q) m -> t b q m", t=PACK, q=RUN)
         for t in range(PACK):
@@ -114,11 +115,11 @@ def tile_picked_twtgatebdif_none_p_kernel(
         def quantize_weight(name, raw, copies):
             codes = tile(name + "_codes", [P, H], U32)
             scales = tile(name + "_scales", [P, H], U8)
-            grouped = [tile("%s_grouped%d" % (name, c), [P, HALF, PACK], BF16) for c in range(2)]
-            for c in range(2):
-                interleave(copies[c], grouped[c][:], raw[c][:])
-            for c in range(2):
-                quantize(codes[:, half(c)], scales[:, half(c)], grouped[c][:])
+            grouped = [tile("%s_grouped%d" % (name, lo), [P, hi - lo, PACK], BF16) for lo, hi, copy in copies]
+            for piece, (lo, hi, copy) in zip(grouped, copies):
+                c = lo // HALF
+                interleave(copy, piece[:], raw[c][:, :, lo - c * HALF : hi - c * HALF])
+                quantize(codes[:, lo:hi], scales[:, lo:hi], piece[:])
             return codes, scales
 
         def product(acc, lhs_codes, lhs_scales, t, rhs_codes, rhs_scales):
@@ -134,14 +135,14 @@ def tile_picked_twtgatebdif_none_p_kernel(
         offs_scales = deal_scales("offs_scales", offs_picked)
         two_words = pick_words("two_words", two_l)
         offs_words = pick_words("offs_words", offs_l)
-        wb_codes, wb_scales = quantize_weight("wb", wb_raw, (nc.scalar.copy, nc.scalar.copy))
-        d_ps = [bank(t, H) for t in range(PACK)]
-        for t in range(PACK):
-            product(d_ps[t][:], two_words, two_scales, t, wb_codes[:], wb_scales[:])
-        wa_codes, wa_scales = quantize_weight("wa", wa_raw, (nc.scalar.copy, nc.vector.tensor_copy))
+        wb_codes, wb_scales = quantize_weight("wb", wb_raw, ((0, 256, nc.scalar.copy), (256, 384, nc.vector.tensor_copy), (384, 512, nc.scalar.copy)))
+        d_sb = [tile("d_sb%d" % t, [P, H], F32) for t in range(PACK)]
+        y_sb = [tile("y_sb%d" % t, [P, H], F32) for t in range(PACK)]
+        wa_codes, wa_scales = quantize_weight("wa", wa_raw, ((0, 256, nc.vector.tensor_copy), (256, 512, nc.vector.tensor_copy)))
         y_ps = [bank(PACK + t, H) for t in range(PACK)]
         for t in range(PACK):
-            product(y_ps[t][:], offs_words, offs_scales, t, wa_codes[:], wa_scales[:])
+            for cols in (half(0), half(1)) if t == 0 else (slice(0, H),):
+                product(y_ps[t][:, cols], offs_words, offs_scales, t, wa_codes[:, cols], wa_scales[:, cols])
 
         def halve_on_scalar(dst, src):
             nc.scalar.activation(dst, src, ACT.Copy, scale=-0.5)
@@ -150,13 +151,13 @@ def tile_picked_twtgatebdif_none_p_kernel(
             nc.vector.tensor_scalar(dst, src, -0.5, None, ALU.mult)
 
         z = [tile("z%d" % c, [P, PACK, HALF], F32) for c in range(2)]
-        d_sb = [tile("d_sb%d" % t, [P, H], F32) for t in range(PACK)]
-        y_sb = [tile("y_sb%d" % t, [P, H], F32) for t in range(PACK)]
 
         def gate(t, c):
             sig = tile("sig%d_%d" % (t, c), [P, HALF], F32, tag="sig", bufs=3)
             if c == 0:
-                nc.scalar.copy(d_sb[t][:], d_ps[t][:])
+                d_ps = bank(t if t < PACK - 1 else PACK, H)
+                product(d_ps[:], two_words, two_scales, t, wb_codes[:], wb_scales[:])
+                nc.scalar.copy(d_sb[t][:], d_ps[:])
             nc.scalar.activation(sig[:], d_sb[t][:].indirect(list_half(n2_l, c)), ACT.Sigmoid)
             if c == 0 and t >= 2:
                 nc.scalar.activation(y_sb[t][:], y_ps[t][:], ACT.Copy, scale=gt_col[t][:])
@@ -169,7 +170,7 @@ def tile_picked_twtgatebdif_none_p_kernel(
 
         for t in range(2):
             nc.vector.tensor_scalar(y_sb[t][:], y_ps[t][:], gt_col[t][:], None, ALU.mult)
-        steps = [(t, c) for c in range(2) for t in range(PACK)]
+        steps = sorted(((t, c) for c in range(2) for t in range(PACK)), key=lambda s: (s[0] + s[1] + s[1], -s[1]))
         gated = [gate(*steps[0])]
         for k in range(1, len(steps)):
             gated.append(gate(*steps[k]))
@@ -182,42 +183,54 @@ def tile_picked_twtgatebdif_none_p_kernel(
         ]
         z_codes = [tile("z_codes%d" % c, [P, HALF], U32) for c in range(2)]
         z_scales = [tile("z_scales%d" % c, [P, HALF], U8) for c in range(2)]
-        w1_grouped = tile("w1_grouped", [P, N, PACK], BF16, tag="d_sb3")
+        w1_on_scalar = tile("w1_on_scalar", [P, N, PACK], BF16, tag="d_sb3")
         w1_codes = tile("w1_codes", [P, N], U32)
         w1_scales = tile("w1_scales", [P, N], U8)
 
         def quantize_w1(u):
             cols = slice(u * P, (u + 1) * P)
-            nc.scalar.copy(
-                w1_grouped[:, cols, :].rearrange("p (b c i) t -> p b c t i", c=2, i=4),
+            if u == 2:
+                copy, grouped = nc.vector.tensor_copy, tile("w1_on_vector", [P, P, PACK], BF16, tag="z_grouped1")[:]
+            else:
+                copy, grouped = nc.scalar.copy, w1_on_scalar[:, cols, :]
+            copy(
+                grouped.rearrange("p (b c i) t -> p b c t i", c=2, i=4),
                 w1_raw[:].rearrange("p t (b u c i) -> p u b c t i", u=PACK, c=2, i=4)[:, u],
             )
-            quantize(w1_codes[:, cols], w1_scales[:, cols], w1_grouped[:, cols, :])
+            quantize(w1_codes[:, cols], w1_scales[:, cols], grouped)
 
         interleave(halve_on_scalar, z_grouped[0][:], z[0][:])
+        interleave(halve_on_vector, z_grouped[1][:], z[1][:])
         quantize(z_codes[0][:], z_scales[0][:], z_grouped[0][:])
         quantize_w1(0)
-        interleave(halve_on_vector, z_grouped[1][:], z[1][:])
-        quantize_w1(1)
         quantize(z_codes[1][:], z_scales[1][:], z_grouped[1][:])
+        quantize_w1(1)
+        quantize_w1(2)
 
         out_rows = out.rearrange("(b u q) n -> u b q n", u=PACK, q=RUN)
         for u in range(PACK):
             h_neg = tile("h_neg%d" % u, [P, H], F32)
             h_pos = [tile("h_pos%d_%d" % (u, c), [P, HALF], F32) for c in range(2)]
-            h_ps = [bank(PACK * c + u, HALF) for c in range(2)]
+            h_ps = [bank(2 * u + c, HALF) for c in range(2)]
             for c in range(2):
                 product(h_ps[c][:], w1_codes, w1_scales, u, z_codes[c][:], z_scales[c][:])
             for c in range(2):
                 nc.scalar.activation(h_neg[:, half(c)], h_ps[c][:], ACT.Copy, scale=-1.0)
             for c in range(2):
                 nc.scalar.copy(h_pos[c][:], h_ps[c][:])
-            if u + 2 < PACK:
-                quantize_w1(u + 2)
+            if u == 0:
+                quantize_w1(PACK - 1)
             res = tile("res%d" % u, [P, H], F32)
-            for c in range(2):
-                nc.vector.tensor_tensor(res[:, half(c)], h_neg[:].indirect(list_half(n3_l, c)), h_pos[c][:], ALU.add)
-                if u == PACK - 1:
-                    nc.sync.dma_start(out_rows[u][:, :, half(c)], res[:, half(c)])
-            if u < PACK - 1:
+            last = u == PACK - 1
+            for lo, hi in ((0, 256), (256, 384), (384, 512)) if last else ((0, 256), (256, 512)):
+                c = lo // HALF
+                nc.vector.tensor_tensor(
+                    res[:, lo:hi],
+                    h_neg[:].indirect(n3_l[:, lo // 16 : hi // 16]),
+                    h_pos[c][:, lo - c * HALF : hi - c * HALF],
+                    ALU.add,
+                )
+                if last:
+                    nc.sync.dma_start(out_rows[u][:, :, lo:hi], res[:, lo:hi])
+            if not last:
                 nc.sync.dma_start(out_rows[u], res[:])

@@ -58,7 +58,8 @@ def tile_picked_twtgatebdif_none_p_kernel(
         offs_l = load_list("offs_l", offs)
         n2_l = load_list("n2_l", n2)
         xs = tile("xs", [P, T], U8)
-        nc.vector.memset(xs[:].bitcast(I32), 0)
+        nc.vector.memset(xs[:, : T // 2].bitcast(I32), 0)
+        nc.gpsimd.memset(xs[:, T // 2 :].bitcast(I32), 0)
         scale_rows = x_scales[0].bitcast(I32).rearrange("(q r) c -> r q c", r=4)
         for r in range(4):
             nc.sync.dma_start(xs[r:P:32, :].bitcast(I32), scale_rows[r])
@@ -156,11 +157,13 @@ def tile_picked_twtgatebdif_none_p_kernel(
             sig = tile("sig%d_%d" % (t, c), [P, HALF], F32, tag="sig", bufs=3)
             if c == 0:
                 d_ps = bank(t if t < PACK - 1 else PACK, H)
-                product(d_ps[:], two_words, two_scales, t, wb_codes[:], wb_scales[:])
+                for cols in (half(0), half(1)) if t == 0 else (slice(0, H),):
+                    product(d_ps[:, cols], two_words, two_scales, t, wb_codes[:, cols], wb_scales[:, cols])
                 nc.scalar.copy(d_sb[t][:], d_ps[:])
             nc.scalar.activation(sig[:], d_sb[t][:].indirect(list_half(n2_l, c)), ACT.Sigmoid)
-            if c == 0 and t >= 2:
-                nc.scalar.activation(y_sb[t][:], y_ps[t][:], ACT.Copy, scale=gt_col[t][:])
+            if c == 0 and t >= 1:
+                cols = half(1) if t == 1 else slice(0, H)
+                nc.scalar.activation(y_sb[t][:, cols], y_ps[t][:, cols], ACT.Copy, scale=gt_col[t][:])
             gated = tile("gated%d_%d" % (t, c), [P, HALF], F32)
             nc.vector.scalar_tensor_tensor(gated[:], y_sb[t][:, half(c)], 2.0, sig[:], ALU.mult, ALU.mult)
             return gated
@@ -168,8 +171,8 @@ def tile_picked_twtgatebdif_none_p_kernel(
         def subtract(t, c, gated):
             nc.vector.tensor_tensor(z[c][:, t, :], y_sb[t][:].indirect(list_half(n1_l, c)), gated[:], ALU.subtract)
 
-        for t in range(2):
-            nc.vector.tensor_scalar(y_sb[t][:], y_ps[t][:], gt_col[t][:], None, ALU.mult)
+        for t, cols in ((0, slice(0, H)), (1, half(0))):
+            nc.vector.tensor_scalar(y_sb[t][:, cols], y_ps[t][:, cols], gt_col[t][:], None, ALU.mult)
         steps = sorted(((t, c) for c in range(2) for t in range(PACK)), key=lambda s: (s[0] + s[1] + s[1], -s[1]))
         gated = [gate(*steps[0])]
         for k in range(1, len(steps)):
@@ -181,8 +184,8 @@ def tile_picked_twtgatebdif_none_p_kernel(
             tile("z_grouped0", [P, HALF, PACK], BF16, tag="sig", bufs=3),
             tile("z_grouped1", [P, HALF, PACK], BF16),
         ]
-        z_codes = [tile("z_codes%d" % c, [P, HALF], U32) for c in range(2)]
-        z_scales = [tile("z_scales%d" % c, [P, HALF], U8) for c in range(2)]
+        z_codes = tile("z_codes", [P, H], U32)
+        z_scales = tile("z_scales", [P, H], U8)
         w1_on_scalar = tile("w1_on_scalar", [P, N, PACK], BF16, tag="d_sb3")
         w1_codes = tile("w1_codes", [P, N], U32)
         w1_scales = tile("w1_scales", [P, N], U8)
@@ -201,33 +204,33 @@ def tile_picked_twtgatebdif_none_p_kernel(
 
         interleave(halve_on_scalar, z_grouped[0][:], z[0][:])
         interleave(halve_on_vector, z_grouped[1][:], z[1][:])
-        quantize(z_codes[0][:], z_scales[0][:], z_grouped[0][:])
+        quantize(z_codes[:, half(0)], z_scales[:, half(0)], z_grouped[0][:])
         quantize_w1(0)
-        quantize(z_codes[1][:], z_scales[1][:], z_grouped[1][:])
+        quantize(z_codes[:, half(1)], z_scales[:, half(1)], z_grouped[1][:])
         quantize_w1(1)
         quantize_w1(2)
 
         out_rows = out.rearrange("(b u q) n -> u b q n", u=PACK, q=RUN)
         for u in range(PACK):
             h_neg = tile("h_neg%d" % u, [P, H], F32)
-            h_pos = [tile("h_pos%d_%d" % (u, c), [P, HALF], F32) for c in range(2)]
-            h_ps = [bank(2 * u + c, HALF) for c in range(2)]
-            for c in range(2):
-                product(h_ps[c][:], w1_codes, w1_scales, u, z_codes[c][:], z_scales[c][:])
-            for c in range(2):
-                nc.scalar.activation(h_neg[:, half(c)], h_ps[c][:], ACT.Copy, scale=-1.0)
-            for c in range(2):
-                nc.scalar.copy(h_pos[c][:], h_ps[c][:])
+            h_pos = tile("h_pos%d" % u, [P, H], F32)
+            parts = (half(0), half(1)) if u < 2 else (slice(0, H),)
+            h_ps = [bank(2 * u + c, cols.stop - cols.start) for c, cols in enumerate(parts)]
+            for acc, cols in zip(h_ps, parts):
+                product(acc[:], w1_codes, w1_scales, u, z_codes[:, cols], z_scales[:, cols])
+            for acc, cols in zip(h_ps, parts):
+                nc.scalar.activation(h_neg[:, cols], acc[:], ACT.Copy, scale=-1.0)
+            for acc, cols in zip(h_ps, parts):
+                nc.scalar.copy(h_pos[:, cols], acc[:])
             if u == 0:
                 quantize_w1(PACK - 1)
             res = tile("res%d" % u, [P, H], F32)
             last = u == PACK - 1
             for lo, hi in ((0, 256), (256, 384), (384, 512)) if last else ((0, 256), (256, 512)):
-                c = lo // HALF
                 nc.vector.tensor_tensor(
                     res[:, lo:hi],
                     h_neg[:].indirect(n3_l[:, lo // 16 : hi // 16]),
-                    h_pos[c][:, lo - c * HALF : hi - c * HALF],
+                    h_pos[:, lo:hi],
                     ALU.add,
                 )
                 if last:

from contextlib import ExitStack

import concourse.mybir as mybir

K, T, S, N, H = 512, 2048, 512, 512, 512
FLOPS = 2 * (K * S * H + K * S * H + S * N * H)

F32 = mybir.dt.float32
BF16 = mybir.dt.bfloat16
I32 = mybir.dt.int32
U32 = mybir.dt.uint32
U16 = mybir.dt.uint16
U8 = mybir.dt.uint8
FP8X4 = mybir.dt.float8_e4m3fn_x4
ALU = mybir.AluOpType
ACT = mybir.ActivationFunctionType

P = 128
PACK = 4
RUN = 8
BLOCKS = P // RUN
HALF = H // 2
LIST_COLS = HALF // 16


def tile_picked_twtgatebdif_none_p_kernel(
    tc, x_words, x_scales, wa, wb, gt, w1, offs, two, n1, n2, n3, out
):
    nc = tc.nc
    with ExitStack() as ctx:
        sb = ctx.enter_context(tc.tile_pool(name="sb", bufs=1))
        psum = ctx.enter_context(tc.psum_pool(name="psum", bufs=1))

        def tile(name, shape, dtype, tag="", bufs=1):
            return sb.tile(shape, dtype, name=name, tag=tag or name, bufs=bufs, align_bytes=64)

        def bank(b, width):
            return psum.tile([P, width], F32, name="bank%d" % b)

        def half(c):
            return slice(c * HALF, (c + 1) * HALF)

        def load_list(name, src):
            lst = tile(name, [P, S // 16], U16)
            nc.sync.dma_start(lst[:], src)
            return lst

        def load_weight(name, src):
            halves = [tile("%s%d" % (name, c), [P, PACK, HALF], F32) for c in range(2)]
            for c in range(2):
                nc.sync.dma_start(halves[c][:], src.rearrange("(p j) n -> p j n", j=PACK)[:, :, half(c)])
            return halves

        def list_half(lst, c):
            return lst[:, c * LIST_COLS : (c + 1) * LIST_COLS]

        two_l = load_list("two_l", two)
        offs_l = load_list("offs_l", offs)
        n2_l = load_list("n2_l", n2)
        xs = tile("xs", [P, T], U8)
        nc.vector.memset(xs[:, : T // 2].bitcast(I32), 0)
        nc.gpsimd.memset(xs[:, T // 2 :].bitcast(I32), 0)
        scale_rows = x_scales[0].bitcast(I32).rearrange("(q r) c -> r q c", r=4)
        for r in range(4):
            nc.sync.dma_start(xs[r:P:32, :].bitcast(I32), scale_rows[r])
        warm = tile("warm", [P, 8], F32)
        nc.vector.memset(warm[:], 0.0)
        warm_out = tile("warm_out", [P, 8], F32)
        nc.scalar.activation(warm_out[:], warm[:], ACT.Sigmoid)

        xw = tile("xw", [P, T], I32)
        nc.sync.dma_start(xw[:], x_words[0].rearrange("p n t -> p (n t)").bitcast(I32))
        wb_raw = load_weight("wb_raw", wb)
        wa_raw = load_weight("wa_raw", wa)
        n1_l = load_list("n1_l", n1)
        gt_rows = gt.rearrange("(b t q) o -> t b q o", t=PACK, q=RUN)
        gt_col = [tile("gt_col%d" % t, [P, 1], F32) for t in range(PACK)]
        for t in range(PACK):
            nc.sync.dma_start(gt_col[t][:], gt_rows[t])
        w1_raw = tile("w1_raw", [P, PACK, N], F32)
        w1_rows = w1.rearrange("(b t q) m -> t b q m", t=PACK, q=RUN)
        for t in range(PACK):
            nc.sync.dma_start(w1_raw[:, t, :], w1_rows[t])
        n3_l = load_list("n3_l", n3)

        def pick_scales(name, lst):
            picked = tile(name + "_picked", [P, S], U8)
            nc.vector.tensor_copy(picked[:], xs[:].indirect(lst[:]))
            return picked

        def deal_scales(name, picked):
            dealt = tile(name, [P, S], U8)
            nc.vector.tensor_copy(
                dealt[:].bitcast(I32).rearrange("p (t b e) -> p t b e", t=PACK, b=BLOCKS),
                picked[:].bitcast(I32).rearrange("p (b t e) -> p t b e", t=PACK, b=BLOCKS),
            )
            return dealt

        def pick_words(name, lst):
            dealt = tile(name, [P, S], U32)
            nc.vector.tensor_copy(
                dealt[:].rearrange("p (t b q) -> p b t q", t=PACK, b=BLOCKS),
                xw[:].bitcast(U32).indirect(lst[:]),
            )
            return dealt

        def interleave(copy, dst, src):
            copy(
                dst.rearrange("p (c i) t -> p c t i", i=4),
                src.rearrange("p t (c i) -> p c t i", i=4),
            )

        def quantize(codes, scales, grouped):
            nc.vector.quantize_mx(out=codes.bitcast(FP8X4), scales=scales, in_=grouped.rearrange("p w j -> p (w j)"))

        def quantize_weight(name, raw, copies):
            codes = tile(name + "_codes", [P, H], U32)
            scales = tile(name + "_scales", [P, H], U8)
            grouped = [tile("%s_grouped%d" % (name, lo), [P, hi - lo, PACK], BF16) for lo, hi, copy in copies]
            for piece, (lo, hi, copy) in zip(grouped, copies):
                c = lo // HALF
                interleave(copy, piece[:], raw[c][:, :, lo - c * HALF : hi - c * HALF])
                quantize(codes[:, lo:hi], scales[:, lo:hi], piece[:])
            return codes, scales

        def product(acc, lhs_codes, lhs_scales, t, rhs_codes, rhs_scales):
            cols = slice(t * P, (t + 1) * P)
            nc.tensor.matmul_mx(
                out=acc, lhsT=lhs_codes[:, cols].bitcast(FP8X4), lhsT_scale=lhs_scales[:, cols],
                rhs=rhs_codes.bitcast(FP8X4), rhs_scale=rhs_scales, start=True, stop=True,
            )

        two_picked = pick_scales("two_scales", two_l)
        offs_picked = pick_scales("offs_scales", offs_l)
        two_scales = deal_scales("two_scales", two_picked)
        offs_scales = deal_scales("offs_scales", offs_picked)
        two_words = pick_words("two_words", two_l)
        offs_words = pick_words("offs_words", offs_l)
        wb_codes, wb_scales = quantize_weight("wb", wb_raw, ((0, 256, nc.scalar.copy), (256, 384, nc.vector.tensor_copy), (384, 512, nc.scalar.copy)))
        d_sb = [tile("d_sb%d" % t, [P, H], F32) for t in range(PACK)]
        y_sb = [tile("y_sb%d" % t, [P, H], F32) for t in range(PACK)]
        wa_codes, wa_scales = quantize_weight("wa", wa_raw, ((0, 256, nc.vector.tensor_copy), (256, 512, nc.vector.tensor_copy)))
        y_ps = [bank(PACK + t, H) for t in range(PACK)]
        for t in range(PACK):
            for cols in (half(0), half(1)) if t == 0 else (slice(0, H),):
                product(y_ps[t][:, cols], offs_words, offs_scales, t, wa_codes[:, cols], wa_scales[:, cols])

        def halve_on_scalar(dst, src):
            nc.scalar.activation(dst, src, ACT.Copy, scale=-0.5)

        def halve_on_vector(dst, src):
            nc.vector.tensor_scalar(dst, src, -0.5, None, ALU.mult)

        z = [tile("z%d" % c, [P, PACK, HALF], F32) for c in range(2)]

        def gate(t, c):
            sig = tile("sig%d_%d" % (t, c), [P, HALF], F32, tag="sig", bufs=3)
            if c == 0:
                d_ps = bank(t if t < PACK - 1 else PACK, H)
                for cols in (half(0), half(1)) if t == 0 else (slice(0, H),):
                    product(d_ps[:, cols], two_words, two_scales, t, wb_codes[:, cols], wb_scales[:, cols])
                nc.scalar.copy(d_sb[t][:], d_ps[:])
            nc.scalar.activation(sig[:], d_sb[t][:].indirect(list_half(n2_l, c)), ACT.Sigmoid)
            if c == 0 and t >= 1:
                cols = half(1) if t == 1 else slice(0, H)
                nc.scalar.activation(y_sb[t][:, cols], y_ps[t][:, cols], ACT.Copy, scale=gt_col[t][:])
            gated = tile("gated%d_%d" % (t, c), [P, HALF], F32)
            nc.vector.scalar_tensor_tensor(gated[:], y_sb[t][:, half(c)], 2.0, sig[:], ALU.mult, ALU.mult)
            return gated

        def subtract(t, c, gated):
            nc.vector.tensor_tensor(z[c][:, t, :], y_sb[t][:].indirect(list_half(n1_l, c)), gated[:], ALU.subtract)

        for t, cols in ((0, slice(0, H)), (1, half(0))):
            nc.vector.tensor_scalar(y_sb[t][:, cols], y_ps[t][:, cols], gt_col[t][:], None, ALU.mult)
        steps = sorted(((t, c) for c in range(2) for t in range(PACK)), key=lambda s: (s[0] + s[1] + s[1], -s[1]))
        gated = [gate(*steps[0])]
        for k in range(1, len(steps)):
            gated.append(gate(*steps[k]))
            subtract(*steps[k - 1], gated[k - 1])
        subtract(*steps[-1], gated[-1])

        z_grouped = [
            tile("z_grouped0", [P, HALF, PACK], BF16, tag="sig", bufs=3),
            tile("z_grouped1", [P, HALF, PACK], BF16),
        ]
        z_codes = tile("z_codes", [P, H], U32)
        z_scales = tile("z_scales", [P, H], U8)
        w1_on_scalar = tile("w1_on_scalar", [P, N, PACK], BF16, tag="d_sb3")
        w1_codes = tile("w1_codes", [P, N], U32)
        w1_scales = tile("w1_scales", [P, N], U8)

        def quantize_w1(u):
            cols = slice(u * P, (u + 1) * P)
            if u == 2:
                copy, grouped = nc.vector.tensor_copy, tile("w1_on_vector", [P, P, PACK], BF16, tag="z_grouped1")[:]
            else:
                copy, grouped = nc.scalar.copy, w1_on_scalar[:, cols, :]
            copy(
                grouped.rearrange("p (b c i) t -> p b c t i", c=2, i=4),
                w1_raw[:].rearrange("p t (b u c i) -> p u b c t i", u=PACK, c=2, i=4)[:, u],
            )
            quantize(w1_codes[:, cols], w1_scales[:, cols], grouped)

        interleave(halve_on_scalar, z_grouped[0][:], z[0][:])
        interleave(halve_on_vector, z_grouped[1][:], z[1][:])
        quantize(z_codes[:, half(0)], z_scales[:, half(0)], z_grouped[0][:])
        quantize_w1(0)
        quantize(z_codes[:, half(1)], z_scales[:, half(1)], z_grouped[1][:])
        quantize_w1(1)
        quantize_w1(2)

        out_rows = out.rearrange("(b u q) n -> u b q n", u=PACK, q=RUN)
        for u in range(PACK):
            h_neg = tile("h_neg%d" % u, [P, H], F32)
            h_pos = tile("h_pos%d" % u, [P, H], F32)
            parts = (half(0), half(1)) if u < 2 else (slice(0, H),)
            h_ps = [bank(2 * u + c, cols.stop - cols.start) for c, cols in enumerate(parts)]
            for acc, cols in zip(h_ps, parts):
                product(acc[:], w1_codes, w1_scales, u, z_codes[:, cols], z_scales[:, cols])
            for acc, cols in zip(h_ps, parts):
                nc.scalar.activation(h_neg[:, cols], acc[:], ACT.Copy, scale=-1.0)
            for acc, cols in zip(h_ps, parts):
                nc.scalar.copy(h_pos[:, cols], acc[:])
            if u == 0:
                quantize_w1(PACK - 1)
            res = tile("res%d" % u, [P, H], F32)
            last = u == PACK - 1
            for lo, hi in ((0, 256), (256, 384), (384, 512)) if last else ((0, 256), (256, 512)):
                nc.vector.tensor_tensor(
                    res[:, lo:hi],
                    h_neg[:].indirect(n3_l[:, lo // 16 : hi // 16]),
                    h_pos[:, lo:hi],
                    ALU.add,
                )
                if last:
                    nc.sync.dma_start(out_rows[u][:, :, lo:hi], res[:, lo:hi])
            if not last:
                nc.sync.dma_start(out_rows[u], res[:])
